import numpy as np
import ml_dtypes


def mxq(x, axis, fmt="e4m3"):
    dtype, down = {"e4m3": (ml_dtypes.float8_e4m3fn, 7), "e5m2": (ml_dtypes.float8_e5m2, 14)}[fmt]
    v = np.moveaxis(np.asarray(x, np.float32).astype(ml_dtypes.bfloat16).astype(np.float64), axis, -1)
    blocks = v.reshape(v.shape[:-1] + (-1, 32))
    amax = np.abs(blocks).max(-1, keepdims=True)
    byte = np.maximum(np.where(amax > 0, np.frexp(amax)[1] - 1 + 127, 0) - down, 1)
    scale = np.exp2(byte - 127.0)
    codes = (blocks / scale).astype(np.float32).astype(dtype).astype(np.float64)
    return np.moveaxis((codes * scale).reshape(v.shape), -1, axis)


WIDE = False


def mx_kscale(k):
    if not WIDE:
        return np.ones(k)
    levels = np.array([10, -10, 5, -5, 0])
    if k % 512:
        return np.exp2(np.random.permutation(np.resize(levels, k // 32))).repeat(32)
    a = np.empty((k // 512, 16))
    for p in range(k // 512):
        a[p, :8] = np.random.permutation(np.resize(levels, 8))
        for g in range(8):
            far = levels[np.abs(levels - a[p, g]) >= 10]
            a[p, g + 8] = far[np.random.randint(len(far))]
    return np.exp2(a.ravel()).repeat(32)


def f64(x):
    return np.asarray(x).astype(np.float64)


def striped(idx):
    return np.tile(idx.reshape(-1, 16).T, (8, 1)).astype(np.uint16)


def unstriped(offs):
    return offs[:16].T.reshape(-1).astype(np.int64)


def pack_weight(w):
    k, n = w.shape
    w = f64(np.asarray(w, np.float32).astype(ml_dtypes.bfloat16)).reshape(k // 32, 32, n)
    amax = np.abs(w).max(1)
    byte = np.clip(np.where(amax > 0, np.frexp(amax)[1] - 1 + 127 - 7, 1), 1, 254)
    scaled = (w * np.exp2(127.0 - byte)[:, None, :]).reshape(k, n).astype(np.float32)
    words = np.ascontiguousarray(scaled.reshape(k // 512, 128, 4, n).transpose(0, 1, 3, 2)).astype(ml_dtypes.float8_e4m3fn).view(np.uint8)
    return words, np.ascontiguousarray(byte.astype(np.uint8).reshape(k // 512, 16, n))


def unpack_weight(words, scales):
    g, p, n, _ = words.shape
    vals = np.ascontiguousarray(words).view(ml_dtypes.float8_e4m3fn).astype(np.float64) * np.repeat(np.exp2(scales.astype(np.float64) - 127.0), 8, axis=1)[..., None]
    return vals.transpose(0, 1, 3, 2).reshape(g * 512, n)


K, T, S, D, N, H = 1024, 2048, 512, 4, 128, 512


def setup_inputs():
    n = np.random.standard_normal
    s = mx_kscale(K)[:, None]
    u = mx_kscale(H)
    packed_xT = pack_weight(n((K, T)) * s)
    return {
        "x_words": packed_xT[0],
        "x_scales": packed_xT[1],
        "hT": (n((K, H)) / np.sqrt(K) / s).astype(np.float32),
        "sw": (np.random.uniform(0.1, 0.5, (H, S))).astype(np.float32),
        "unit": (np.random.uniform(0.6, 1.4, (H, 1)) * u[:, None]).astype(np.float32),
        "w1": (n((H, N)) / np.sqrt(H) / u[:, None]).astype(np.float32),
        "offs": striped(np.random.permutation(T)[:S]),
        "rec": striped(np.random.permutation(S)),
    }


def reference(x_words, x_scales, hT, sw, unit, w1, offs, rec):
    hTq = mxq(f64(hT), 0, "e4m3")
    xq = unpack_weight(x_words, x_scales)[:, unstriped(offs)]
    y = hTq.T @ xq
    em = np.exp(1.1 * np.tanh(y))
    er = em[:, unstriped(rec)]
    avg = em.mean(axis=1, keepdims=True)
    fwd = (-1.0 * f64(sw) + 1.0) * er + f64(sw) * avg
    post = em * fwd
    ps = post.reshape(len(post), -1, D).sum(axis=2)
    nrm = post / (np.repeat(ps, D, axis=1) + 0.2)
    hid = f64(unit) * nrm
    return mxq(f64(w1), 0, "e4m3").T @ mxq(hid, 0, "e4m3")

@@ -1,0 +1,177 @@
+from contextlib import ExitStack
+
+import concourse.mybir as mybir
+
+K, T, S, D, N, H = 1024, 2048, 512, 4, 128, 512
+FLOPS = 2 * K * H * S + 2 * H * N * S
+
+F32 = mybir.dt.float32
+BF16 = mybir.dt.bfloat16
+I32 = mybir.dt.int32
+U32 = mybir.dt.uint32
+U16 = mybir.dt.uint16
+U8 = mybir.dt.uint8
+FP8X4 = mybir.dt.float8_e4m3fn_x4
+ACT = mybir.ActivationFunctionType
+ALU = mybir.AluOpType
+
+P = 128
+PACK = 4
+PASSES = K // (P * PACK)
+GROUPS = S // D
+OUT_CHUNKS = 2
+
+
+def tile_picked_ypopgn_post_p_kernel(tc, x_words, x_scales, hT, sw, unit, w1, offs, rec, out):
+    nc = tc.nc
+    with ExitStack() as ctx:
+        sb = ctx.enter_context(tc.tile_pool(name="sb", bufs=1))
+        psum = ctx.enter_context(tc.psum_pool(name="psum", bufs=1))
+
+        offs_t = sb.tile([P, S // 16], U16, name="offs_t")
+        rec_t = sb.tile([P, S // 16], U16, name="rec_t")
+        xs_all = sb.tile([P, T], U8, name="xs_all", align_bytes=64)
+        xs_in = sb.tile([P, T // 4], I32, name="xs_in")
+        h_raw = [sb.tile([P, PACK, H], F32, name=f"h_raw{o}") for o in range(PASSES)]
+        xw_all = [sb.tile([P, T], U32, name=f"xw_all{o}", align_bytes=64) for o in range(PASSES)]
+        sw_t = [sb.tile([P, S], F32, name=f"sw{t}") for t in range(PACK)]
+        unit_t = sb.tile([P, PACK], F32, name="unit_t")
+        w_raw = sb.tile([P, PACK, N], F32, name="w_raw")
+        h_rows = hT.rearrange("(o p j) c -> o p j c", o=PASSES, j=PACK)
+        nc.sync.dma_start(out=h_raw[0][:], in_=h_rows[0])
+        for q in range(4):
+            nc.sync.dma_start(out=xs_in[32 * q : 32 * q + 8, :], in_=x_scales[:, 4 * q : 4 * q + 4, :].bitcast(I32))
+        nc.sync.dma_start(offs_t[:], offs)
+        nc.sync.dma_start(out=h_raw[1][:], in_=h_rows[1])
+        for o in range(PASSES):
+            nc.sync.dma_start(out=xw_all[o][:].bitcast(I32), in_=x_words[o].rearrange("p n r -> p (n r)").bitcast(I32))
+        nc.sync.dma_start(out=w_raw[:], in_=w1.rearrange("(p j) m -> p j m", j=PACK))
+        nc.sync.dma_start(rec_t[:], rec)
+        sw_rows = sw.rearrange("(p t) j -> p t j", t=PACK)
+        for t in range(PACK):
+            nc.sync.dma_start(out=sw_t[t][:], in_=sw_rows[:, t, :])
+        nc.sync.dma_start(out=unit_t[:], in_=unit.rearrange("(p t) o -> p (t o)", t=PACK))
+
+        nc.vector.memset(xs_all[:].bitcast(I32), 0)
+        for q in range(4):
+            nc.vector.tensor_copy(xs_all[32 * q : 32 * q + 8, :].bitcast(I32), xs_in[32 * q : 32 * q + 8, :])
+
+        h_codes = [sb.tile([P, H], U32, name=f"h_codes{o}", align_bytes=64) for o in range(PASSES)]
+        h_scales = [sb.tile([P, H], U8, name=f"h_scales{o}", align_bytes=64) for o in range(PASSES)]
+        for o in range(PASSES):
+            src = h_raw[o][:].rearrange("p j (m t) -> p m j t", t=PACK)
+            for half in range(2):
+                h_bf = sb.tile([P, 2, P, PACK], BF16, name=f"h_bf{o}{half}", align_bytes=64)
+                dst = h_bf[:].rearrange("p t m j -> p m j t")
+                if half == 0:
+                    nc.vector.tensor_copy(out=dst, in_=src[:, :, :, 0:2])
+                else:
+                    nc.scalar.activation(dst, src[:, :, :, 2:4], ACT.Copy)
+                cols = slice(256 * half, 256 * (half + 1))
+                nc.vector.quantize_mx(
+                    out=h_codes[o][:, cols].bitcast(FP8X4),
+                    scales=h_scales[o][:, cols],
+                    in_=h_bf[:].rearrange("p t m j -> p (t m j)"),
+                )
+
+        xs = sb.tile([P, S], U8, name="xs", align_bytes=64)
+        nc.vector.tensor_copy(xs[:], xs_all[:].indirect(offs_t[:]))
+        xw = [sb.tile([P, S], U32, name=f"xw{o}", align_bytes=64) for o in range(PASSES)]
+        halves = [slice(0, S // 2), slice(S // 2, S)]
+        pieces = [(0, halves[0]), (0, halves[1])] + [(t, slice(0, S)) for t in range(1, PACK)]
+        y = [psum.tile([P, c.stop - c.start], F32, name=f"y{n}") for n, (t, c) in enumerate(pieces)]
+        for o in range(PASSES):
+            for h in range(2):
+                nc.vector.tensor_copy(xw[o][:, halves[h]], xw_all[o][:].indirect(offs_t[:, 16 * h : 16 * (h + 1)]))
+            for n, (t, c) in enumerate(pieces):
+                cols = slice(P * t, P * (t + 1))
+                nc.tensor.matmul_mx(
+                    out=y[n][:],
+                    lhsT=h_codes[o][:, cols].bitcast(FP8X4),
+                    lhsT_scale=h_scales[o][:, cols],
+                    rhs=xw[o][:, c].bitcast(FP8X4),
+                    rhs_scale=xs[4 * o : P, c],
+                    start=(o == 0),
+                    stop=(o == PASSES - 1),
+                )
+
+        w_bf = sb.tile([P, N, PACK], BF16, name="w_bf", align_bytes=64)
+        nc.vector.tensor_copy(
+            w_bf[:].rearrange("p (c i) j -> p c j i", i=4), w_raw[:].rearrange("p j (c i) -> p c j i", i=4)
+        )
+        w_codes = sb.tile([P, N], U32, name="w_codes", align_bytes=64)
+        w_scales = sb.tile([P, N], U8, name="w_scales", align_bytes=64)
+        nc.vector.quantize_mx(out=w_codes[:].bitcast(FP8X4), scales=w_scales[:], in_=w_bf[:].rearrange("p m j -> p (m j)"))
+
+        total = sb.tile([P, PACK], F32, name="total")
+        avg = sb.tile([P, PACK], F32, name="avg")
+        post = sb.tile([P, PACK, S], F32, name="post")
+        den = sb.tile([P, PACK, GROUPS], F32, name="den")
+        for t in range(PACK):
+            col = slice(t, t + 1)
+            stay = sb.tile([P, S], F32, name=f"stay{t}", tag=f"stay{t}", align_bytes=64)
+            nc.vector.tensor_scalar(stay[:], sw_t[t][:], -1.0, 1.0, ALU.mult, ALU.add)
+            em_th = sb.tile([P, 2 * S], F32, name=f"em_th{t}")
+            em = em_th[:, 0:S]
+            th = em_th[:, S : 2 * S]
+            for n, (tn, c) in enumerate(pieces):
+                if tn == t:
+                    nc.scalar.activation(em_th[:, S + c.start : S + c.stop], y[n][:], ACT.Tanh)
+            nc.scalar.activation(em, th, ACT.Exp, scale=1.1, accum_out=total[:, col])
+            nc.gpsimd.tensor_scalar(avg[:, col], total[:, col], 1.0 / S, 0.0, ALU.mult, ALU.add)
+            er = sb.tile([P, S], F32, name=f"er{t}")
+            kept = sb.tile([P, S], F32, name=f"kept{t}")
+            pairs = sb.tile([P, GROUPS, 2], F32, name=f"pairs{t}")
+            quads = post[:, t, :].rearrange("p (v d) -> p v d", d=D)
+            vhalves = [slice(0, GROUPS // 2), slice(GROUPS // 2, GROUPS)]
+            for h in range(2):
+                picked = em_th[:].indirect(rec_t[:, 16 * h : 16 * (h + 1)])
+                if t == 0 or (t, h) == (3, 1):
+                    nc.vector.tensor_copy(er[:, halves[h]], picked)
+                else:
+                    nc.scalar.activation(er[:, halves[h]], picked, ACT.Copy)
+            for c in halves:
+                nc.vector.scalar_tensor_tensor(kept[:, c], er[:, c], avg[:, col], stay[:, c], ALU.subtract, ALU.mult)
+            for c in halves:
+                nc.vector.scalar_tensor_tensor(post[:, t, c], kept[:, c], avg[:, col], em_th[:, c], ALU.add, ALU.mult)
+            for v in vhalves:
+                nc.vector.tensor_tensor(pairs[:, v, :], quads[:, v, 0:2], quads[:, v, 2:4], ALU.add)
+            for v in vhalves:
+                nc.vector.scalar_tensor_tensor(den[:, t, v], pairs[:, v, 0], 0.2, pairs[:, v, 1], ALU.add, ALU.add)
+
+        sign = sb.tile([P, PACK, GROUPS], F32, name="sign")
+        root = sb.tile([P, PACK, GROUPS], F32, name="root")
+        inv = sb.tile([P, PACK, GROUPS], F32, name="inv")
+        factor = sb.tile([P, PACK, GROUPS], F32, name="factor")
+        width = S // OUT_CHUNKS
+        for c in range(OUT_CHUNKS):
+            cols = slice(width * c, width * (c + 1))
+            vs = slice(width * c // D, width * (c + 1) // D)
+            nc.scalar.activation(root[:, :, vs], den[:, :, vs], ACT.Abs_reciprocal_sqrt)
+            nc.scalar.activation(sign[:, :, vs], den[:, :, vs], ACT.Sign)
+            nc.scalar.activation(inv[:, :, vs], root[:, :, vs], ACT.Square)
+            for t in range(PACK):
+                nc.vector.scalar_tensor_tensor(factor[:, t, vs], inv[:, t, vs], unit_t[:, t : t + 1], sign[:, t, vs], ALU.mult, ALU.mult)
+            hid = sb.tile([P, width, PACK], BF16, name=f"hid{c}", align_bytes=64)
+            nc.vector.tensor_tensor(
+                hid[:].rearrange("p (v d) t -> p v t d", d=D),
+                post[:, :, cols].rearrange("p t (v d) -> p v t d", d=D),
+                factor[:, :, vs].rearrange("p t v -> p v t").unsqueeze(3).to_broadcast([P, width // D, PACK, D]),
+                ALU.mult,
+            )
+            hid_codes = sb.tile([P, width], U32, name=f"hid_codes{c}", align_bytes=64)
+            hid_scales = sb.tile([P, width], U8, name=f"hid_scales{c}", align_bytes=64)
+            nc.vector.quantize_mx(out=hid_codes[:].bitcast(FP8X4), scales=hid_scales[:], in_=hid[:].rearrange("p j t -> p (j t)"))
+            acc = psum.tile([P, width], F32, name=f"acc{c}")
+            nc.tensor.matmul_mx(
+                out=acc[:],
+                lhsT=w_codes[:].bitcast(FP8X4),
+                lhsT_scale=w_scales[:],
+                rhs=hid_codes[:].bitcast(FP8X4),
+                rhs_scale=hid_scales[:],
+                start=True,
+                stop=True,
+            )
+            res = sb.tile([P, width], F32, name=f"res{c}")
+            nc.scalar.copy(res[:], acc[:])
+            nc.sync.dma_start(out=out[:, cols], in_=res[:])

@@ -104,40 +104,50 @@ def tile_picked_ypopgn_post_p_kernel(tc, x_words, x_scales, hT, sw, unit, w1, of
         nc.vector.quantize_mx(out=w_codes[:].bitcast(FP8X4), scales=w_scales[:], in_=w_bf[:].rearrange("p m j -> p (m j)"))
 
         total = sb.tile([P, PACK], F32, name="total")
-        avg = sb.tile([P, PACK], F32, name="avg")
         post = sb.tile([P, PACK, S], F32, name="post")
         den = sb.tile([P, PACK, GROUPS], F32, name="den")
+        vhalves = [slice(0, GROUPS // 2), slice(GROUPS // 2, GROUPS)]
+        on_vector = [(0, 0), (0, 1), (3, 1)]
         for t in range(PACK):
             col = slice(t, t + 1)
-            stay = sb.tile([P, S], F32, name=f"stay{t}", tag=f"stay{t}", align_bytes=64)
-            nc.vector.tensor_scalar(stay[:], sw_t[t][:], -1.0, 1.0, ALU.mult, ALU.add)
-            em_th = sb.tile([P, 2 * S], F32, name=f"em_th{t}")
-            em = em_th[:, 0:S]
-            th = em_th[:, S : 2 * S]
+            th = sb.tile([P, S], F32, name=f"th{t}")
+            em = sb.tile([P, S], F32, name=f"em{t}")
             for n, (tn, c) in enumerate(pieces):
                 if tn == t:
-                    nc.scalar.activation(em_th[:, S + c.start : S + c.stop], y[n][:], ACT.Tanh)
-            nc.scalar.activation(em, th, ACT.Exp, scale=1.1, accum_out=total[:, col])
-            nc.gpsimd.tensor_scalar(avg[:, col], total[:, col], 1.0 / S, 0.0, ALU.mult, ALU.add)
+                    nc.scalar.activation(th[:, c], y[n][:], ACT.Tanh)
+            nc.scalar.activation(em[:], th[:], ACT.Exp, scale=1.1, accum_out=total[:, col])
+            avg = sb.tile([P, 1], F32, name=f"avg{t}")
+            if t == 0:
+                nc.vector.tensor_scalar(avg[:], total[:, col], 1.0 / S, None, ALU.mult)
+            elif t == 3:
+                nc.scalar.activation(avg[:], total[:, col], ACT.Copy, scale=1.0 / S)
+            stay = sb.tile([P, S], F32, name=f"stay{t}")
             er = sb.tile([P, S], F32, name=f"er{t}")
             kept = sb.tile([P, S], F32, name=f"kept{t}")
             pairs = sb.tile([P, GROUPS, 2], F32, name=f"pairs{t}")
             quads = post[:, t, :].rearrange("p (v d) -> p v d", d=D)
-            vhalves = [slice(0, GROUPS // 2), slice(GROUPS // 2, GROUPS)]
+            if t == 0:
+                nc.vector.tensor_scalar(stay[:], sw_t[t][:], -float(S), float(S), ALU.mult, ALU.add)
+            elif t == 3:
+                nc.vector.tensor_scalar(stay[:, halves[0]], sw_t[t][:, halves[0]], -1.0, 1.0, ALU.mult, ALU.add)
+                nc.vector.tensor_scalar(stay[:, halves[1]], sw_t[t][:, halves[1]], -float(S), float(S), ALU.mult, ALU.add)
+            else:
+                nc.vector.tensor_scalar(stay[:], sw_t[t][:], -1.0, 1.0, ALU.mult, ALU.add)
             for h in range(2):
-                picked = em_th[:].indirect(rec_t[:, 16 * h : 16 * (h + 1)])
-                if t == 0 or (t, h) == (3, 1):
+                picked = em[:].indirect(rec_t[:, 16 * h : 16 * (h + 1)])
+                if (t, h) in on_vector:
                     nc.vector.tensor_copy(er[:, halves[h]], picked)
                 else:
-                    nc.scalar.activation(er[:, halves[h]], picked, ACT.Copy)
+                    nc.scalar.activation(er[:, halves[h]], picked, ACT.Copy, scale=float(S))
+            for h, c in enumerate(halves):
+                centre = avg[:] if (t, h) in on_vector else total[:, col]
+                nc.vector.scalar_tensor_tensor(kept[:, c], er[:, c], centre, stay[:, c], ALU.subtract, ALU.mult)
             for c in halves:
-                nc.vector.scalar_tensor_tensor(kept[:, c], er[:, c], avg[:, col], stay[:, c], ALU.subtract, ALU.mult)
-            for c in halves:
-                nc.vector.scalar_tensor_tensor(post[:, t, c], kept[:, c], avg[:, col], em_th[:, c], ALU.add, ALU.mult)
+                nc.vector.scalar_tensor_tensor(post[:, t, c], kept[:, c], total[:, col], em[:, c], ALU.add, ALU.mult)
             for v in vhalves:
                 nc.vector.tensor_tensor(pairs[:, v, :], quads[:, v, 0:2], quads[:, v, 2:4], ALU.add)
             for v in vhalves:
-                nc.vector.scalar_tensor_tensor(den[:, t, v], pairs[:, v, 0], 0.2, pairs[:, v, 1], ALU.add, ALU.add)
+                nc.vector.scalar_tensor_tensor(den[:, t, v], pairs[:, v, 0], 0.2 * S, pairs[:, v, 1], ALU.add, ALU.add)
 
         sign = sb.tile([P, PACK, GROUPS], F32, name="sign")
         root = sb.tile([P, PACK, GROUPS], F32, name="root")
@@ -150,15 +160,20 @@ def tile_picked_ypopgn_post_p_kernel(tc, x_words, x_scales, hT, sw, unit, w1, of
             nc.scalar.activation(root[:, :, vs], den[:, :, vs], ACT.Abs_reciprocal_sqrt)
             nc.scalar.activation(sign[:, :, vs], den[:, :, vs], ACT.Sign)
             nc.scalar.activation(inv[:, :, vs], root[:, :, vs], ACT.Square)
+            nc.vector.tensor_tensor(factor[:, :, vs], inv[:, :, vs], sign[:, :, vs], ALU.mult)
+            planes = sb.tile([P, PACK, width], BF16, name=f"planes{c}")
             for t in range(PACK):
-                nc.vector.scalar_tensor_tensor(factor[:, t, vs], inv[:, t, vs], unit_t[:, t : t + 1], sign[:, t, vs], ALU.mult, ALU.mult)
+                nc.vector.scalar_tensor_tensor(
+                    planes[:, t, :].rearrange("p (v d) -> p v d", d=D),
+                    post[:, t, cols].rearrange("p (v d) -> p v d", d=D),
+                    unit_t[:, t : t + 1],
+                    factor[:, t, vs].unsqueeze(2).to_broadcast([P, width // D, D]),
+                    ALU.mult,
+                    ALU.mult,
+                )
             hid = sb.tile([P, width, PACK], BF16, name=f"hid{c}", align_bytes=64)
-            nc.vector.tensor_tensor(
-                hid[:].rearrange("p (v d) t -> p v t d", d=D),
-                post[:, :, cols].rearrange("p t (v d) -> p v t d", d=D),
-                factor[:, :, vs].rearrange("p t v -> p v t").unsqueeze(3).to_broadcast([P, width // D, PACK, D]),
-                ALU.mult,
-            )
+            weave = nc.scalar.copy if c == 0 else nc.vector.tensor_copy
+            weave(hid[:].rearrange("p (g i) t -> p g t i", i=4), planes[:].rearrange("p t (g i) -> p g t i", i=4))
             hid_codes = sb.tile([P, width], U32, name=f"hid_codes{c}", align_bytes=64)
             hid_scales = sb.tile([P, width], U8, name=f"hid_scales{c}", align_bytes=64)
             nc.vector.quantize_mx(out=hid_codes[:].bitcast(FP8X4), scales=hid_scales[:], in_=hid[:].rearrange("p j t -> p (j t)"))

@@ -31,7 +31,10 @@ def tile_picked_ypopgn_post_p_kernel(tc, x_words, x_scales, hT, sw, unit, w1, of
         offs_t = sb.tile([P, S // 16], U16, name="offs_t")
         rec_t = sb.tile([P, S // 16], U16, name="rec_t")
         xs_all = sb.tile([P, T], U8, name="xs_all", align_bytes=64)
-        xs_in = sb.tile([P, T // 4], I32, name="xs_in")
+        nc.scalar.dma_start(out=xs_all[0:32, :].bitcast(I32), in_=x_scales.rearrange("o b n -> b o n").bitcast(I32))
+        nc.sync.dma_start(offs_t[:], offs)
+        nc.vector.memset(xs_all[32:64, :].bitcast(I32), 0)
+        nc.vector.memset(xs_all[64:128, :].bitcast(I32), 0)
         h_raw = [sb.tile([P, PACK, H], F32, name=f"h_raw{o}") for o in range(PASSES)]
         xw_all = [sb.tile([P, T], U32, name=f"xw_all{o}", align_bytes=64) for o in range(PASSES)]
         sw_t = [sb.tile([P, S], F32, name=f"sw{t}") for t in range(PACK)]
@@ -39,9 +42,6 @@ def tile_picked_ypopgn_post_p_kernel(tc, x_words, x_scales, hT, sw, unit, w1, of
         w_raw = sb.tile([P, PACK, N], F32, name="w_raw")
         h_rows = hT.rearrange("(o p j) c -> o p j c", o=PASSES, j=PACK)
         nc.sync.dma_start(out=h_raw[0][:], in_=h_rows[0])
-        for q in range(4):
-            nc.sync.dma_start(out=xs_in[32 * q : 32 * q + 8, :], in_=x_scales[:, 4 * q : 4 * q + 4, :].bitcast(I32))
-        nc.sync.dma_start(offs_t[:], offs)
         nc.sync.dma_start(out=h_raw[1][:], in_=h_rows[1])
         for o in range(PASSES):
             nc.sync.dma_start(out=xw_all[o][:].bitcast(I32), in_=x_words[o].rearrange("p n r -> p (n r)").bitcast(I32))
@@ -52,9 +52,11 @@ def tile_picked_ypopgn_post_p_kernel(tc, x_words, x_scales, hT, sw, unit, w1, of
             nc.sync.dma_start(out=sw_t[t][:], in_=sw_rows[:, t, :])
         nc.sync.dma_start(out=unit_t[:], in_=unit.rearrange("(p t) o -> p (t o)", t=PACK))
 
-        nc.vector.memset(xs_all[:].bitcast(I32), 0)
+        xs_picked = sb.tile([P, S], U8, name="xs_picked", align_bytes=64)
+        nc.vector.tensor_copy(xs_picked[:], xs_all[:].indirect(offs_t[:]))
+        xs = sb.tile([P, PASSES, S], U8, name="xs", align_bytes=64)
         for q in range(4):
-            nc.vector.tensor_copy(xs_all[32 * q : 32 * q + 8, :].bitcast(I32), xs_in[32 * q : 32 * q + 8, :])
+            nc.gpsimd.dma_start(out=xs[32 * q : 32 * q + 4, :, :].bitcast(I32), in_=xs_picked[8 * q : 8 * q + 8, :].bitcast(I32))
 
         h_codes = [sb.tile([P, H], U32, name=f"h_codes{o}", align_bytes=64) for o in range(PASSES)]
         h_scales = [sb.tile([P, H], U8, name=f"h_scales{o}", align_bytes=64) for o in range(PASSES)]
@@ -74,8 +76,6 @@ def tile_picked_ypopgn_post_p_kernel(tc, x_words, x_scales, hT, sw, unit, w1, of
                     in_=h_bf[:].rearrange("p t m j -> p (t m j)"),
                 )
 
-        xs = sb.tile([P, S], U8, name="xs", align_bytes=64)
-        nc.vector.tensor_copy(xs[:], xs_all[:].indirect(offs_t[:]))
         xw = [sb.tile([P, S], U32, name=f"xw{o}", align_bytes=64) for o in range(PASSES)]
         halves = [slice(0, S // 2), slice(S // 2, S)]
         pieces = [(0, halves[0]), (0, halves[1])] + [(t, slice(0, S)) for t in range(1, PACK)]
@@ -83,14 +83,15 @@ def tile_picked_ypopgn_post_p_kernel(tc, x_words, x_scales, hT, sw, unit, w1, of
         for o in range(PASSES):
             for h in range(2):
                 nc.vector.tensor_copy(xw[o][:, halves[h]], xw_all[o][:].indirect(offs_t[:, 16 * h : 16 * (h + 1)]))
-            for n, (t, c) in enumerate(pieces):
-                cols = slice(P * t, P * (t + 1))
+        for n, (t, c) in enumerate(pieces):
+            cols = slice(P * t, P * (t + 1))
+            for o in range(PASSES):
                 nc.tensor.matmul_mx(
                     out=y[n][:],
                     lhsT=h_codes[o][:, cols].bitcast(FP8X4),
                     lhsT_scale=h_scales[o][:, cols],
                     rhs=xw[o][:, c].bitcast(FP8X4),
-                    rhs_scale=xs[4 * o : P, c],
+                    rhs_scale=xs[:, o, c],
                     start=(o == 0),
                     stop=(o == PASSES - 1),
                 )
@@ -107,7 +108,7 @@ def tile_picked_ypopgn_post_p_kernel(tc, x_words, x_scales, hT, sw, unit, w1, of
         post = sb.tile([P, PACK, S], F32, name="post")
         den = sb.tile([P, PACK, GROUPS], F32, name="den")
         vhalves = [slice(0, GROUPS // 2), slice(GROUPS // 2, GROUPS)]
-        on_vector = [(0, 0), (0, 1), (3, 1)]
+        on_vector = [(0, 0), (0, 1)]
         for t in range(PACK):
             col = slice(t, t + 1)
             th = sb.tile([P, S], F32, name=f"th{t}")
@@ -116,11 +117,9 @@ def tile_picked_ypopgn_post_p_kernel(tc, x_words, x_scales, hT, sw, unit, w1, of
                 if tn == t:
                     nc.scalar.activation(th[:, c], y[n][:], ACT.Tanh)
             nc.scalar.activation(em[:], th[:], ACT.Exp, scale=1.1, accum_out=total[:, col])
-            avg = sb.tile([P, 1], F32, name=f"avg{t}")
             if t == 0:
+                avg = sb.tile([P, 1], F32, name="avg")
                 nc.vector.tensor_scalar(avg[:], total[:, col], 1.0 / S, None, ALU.mult)
-            elif t == 3:
-                nc.scalar.activation(avg[:], total[:, col], ACT.Copy, scale=1.0 / S)
             stay = sb.tile([P, S], F32, name=f"stay{t}")
             er = sb.tile([P, S], F32, name=f"er{t}")
             kept = sb.tile([P, S], F32, name=f"kept{t}")
@@ -128,9 +127,6 @@ def tile_picked_ypopgn_post_p_kernel(tc, x_words, x_scales, hT, sw, unit, w1, of
             quads = post[:, t, :].rearrange("p (v d) -> p v d", d=D)
             if t == 0:
                 nc.vector.tensor_scalar(stay[:], sw_t[t][:], -float(S), float(S), ALU.mult, ALU.add)
-            elif t == 3:
-                nc.vector.tensor_scalar(stay[:, halves[0]], sw_t[t][:, halves[0]], -1.0, 1.0, ALU.mult, ALU.add)
-                nc.vector.tensor_scalar(stay[:, halves[1]], sw_t[t][:, halves[1]], -float(S), float(S), ALU.mult, ALU.add)
             else:
                 nc.vector.tensor_scalar(stay[:], sw_t[t][:], -1.0, 1.0, ALU.mult, ALU.add)
             for h in range(2):
@@ -153,27 +149,24 @@ def tile_picked_ypopgn_post_p_kernel(tc, x_words, x_scales, hT, sw, unit, w1, of
         root = sb.tile([P, PACK, GROUPS], F32, name="root")
         inv = sb.tile([P, PACK, GROUPS], F32, name="inv")
         factor = sb.tile([P, PACK, GROUPS], F32, name="factor")
-        width = S // OUT_CHUNKS
-        for c in range(OUT_CHUNKS):
-            cols = slice(width * c, width * (c + 1))
-            vs = slice(width * c // D, width * (c + 1) // D)
+        for vs in vhalves:
             nc.scalar.activation(root[:, :, vs], den[:, :, vs], ACT.Abs_reciprocal_sqrt)
             nc.scalar.activation(sign[:, :, vs], den[:, :, vs], ACT.Sign)
             nc.scalar.activation(inv[:, :, vs], root[:, :, vs], ACT.Square)
-            nc.vector.tensor_tensor(factor[:, :, vs], inv[:, :, vs], sign[:, :, vs], ALU.mult)
-            planes = sb.tile([P, PACK, width], BF16, name=f"planes{c}")
-            for t in range(PACK):
-                nc.vector.scalar_tensor_tensor(
-                    planes[:, t, :].rearrange("p (v d) -> p v d", d=D),
-                    post[:, t, cols].rearrange("p (v d) -> p v d", d=D),
-                    unit_t[:, t : t + 1],
-                    factor[:, t, vs].unsqueeze(2).to_broadcast([P, width // D, D]),
-                    ALU.mult,
-                    ALU.mult,
-                )
+        for c, cols in enumerate([slice(0, 256), slice(256, 384), slice(384, 512)]):
+            width = cols.stop - cols.start
+            vs = slice(cols.start // D, cols.stop // D)
+            if c < 2:
+                for t in range(PACK):
+                    v = vhalves[c]
+                    nc.vector.scalar_tensor_tensor(factor[:, t, v], inv[:, t, v], unit_t[:, t : t + 1], sign[:, t, v], ALU.mult, ALU.mult)
             hid = sb.tile([P, width, PACK], BF16, name=f"hid{c}", align_bytes=64)
-            weave = nc.scalar.copy if c == 0 else nc.vector.tensor_copy
-            weave(hid[:].rearrange("p (g i) t -> p g t i", i=4), planes[:].rearrange("p t (g i) -> p g t i", i=4))
+            nc.vector.tensor_tensor(
+                hid[:].rearrange("p (v d) t -> p v t d", d=D),
+                post[:, :, cols].rearrange("p t (v d) -> p v t d", d=D),
+                factor[:, :, vs].rearrange("p t v -> p v t").unsqueeze(3).to_broadcast([P, width // D, PACK, D]),
+                ALU.mult,
+            )
             hid_codes = sb.tile([P, width], U32, name=f"hid_codes{c}", align_bytes=64)
             hid_scales = sb.tile([P, width], U8, name=f"hid_scales{c}", align_bytes=64)
             nc.vector.quantize_mx(out=hid_codes[:].bitcast(FP8X4), scales=hid_scales[:], in_=hid[:].rearrange("p j t -> p (j t)"))

@@ -18,8 +18,17 @@ ALU = mybir.AluOpType
 P = 128
 PACK = 4
 PASSES = K // (P * PACK)
+BLOCKS = P * PACK // 32
 GROUPS = S // D
-OUT_CHUNKS = 2
+MX_ALIGN = 64
+
+ENTRIES = [slice(0, S // 2), slice(S // 2, S)]
+LIST_COLUMNS = [slice(0, S // 32), slice(S // 32, S // 16)]
+GROUP_HALVES = [slice(0, GROUPS // 2), slice(GROUPS // 2, GROUPS)]
+
+PIECE_PAIRS = [[(0, 0), (0, 1)], [(1, 0), (1, 1)], [(2, 0), (3, 0)], [(2, 1), (3, 1)]]
+VECTOR_LOOKUPS = [(0, 0), (0, 1), (1, 0)]
+OUT_CHUNKS = [slice(0, 256), slice(256, 384), slice(384, 512)]
 
 
 def tile_picked_ypopgn_post_p_kernel(tc, x_words, x_scales, hT, sw, unit, w1, offs, rec, out):
@@ -28,149 +37,161 @@ def tile_picked_ypopgn_post_p_kernel(tc, x_words, x_scales, hT, sw, unit, w1, of
         sb = ctx.enter_context(tc.tile_pool(name="sb", bufs=1))
         psum = ctx.enter_context(tc.psum_pool(name="psum", bufs=1))
 
-        offs_t = sb.tile([P, S // 16], U16, name="offs_t")
-        rec_t = sb.tile([P, S // 16], U16, name="rec_t")
-        xs_all = sb.tile([P, T], U8, name="xs_all", align_bytes=64)
-        nc.scalar.dma_start(out=xs_all[0:32, :].bitcast(I32), in_=x_scales.rearrange("o b n -> b o n").bitcast(I32))
-        nc.sync.dma_start(offs_t[:], offs)
-        nc.vector.memset(xs_all[32:64, :].bitcast(I32), 0)
-        nc.vector.memset(xs_all[64:128, :].bitcast(I32), 0)
-        h_raw = [sb.tile([P, PACK, H], F32, name=f"h_raw{o}") for o in range(PASSES)]
-        xw_all = [sb.tile([P, T], U32, name=f"xw_all{o}", align_bytes=64) for o in range(PASSES)]
-        sw_t = [sb.tile([P, S], F32, name=f"sw{t}") for t in range(PACK)]
-        unit_t = sb.tile([P, PACK], F32, name="unit_t")
-        w_raw = sb.tile([P, PACK, N], F32, name="w_raw")
-        h_rows = hT.rearrange("(o p j) c -> o p j c", o=PASSES, j=PACK)
-        nc.sync.dma_start(out=h_raw[0][:], in_=h_rows[0])
-        nc.sync.dma_start(out=h_raw[1][:], in_=h_rows[1])
+        def quantise(values, codes, scales):
+            nc.vector.quantize_mx(out=codes.bitcast(FP8X4), scales=scales, in_=values)
+
+        scale_rows = PASSES * BLOCKS
+        x_scales_all = sb.tile([P, T], U8, name="x_scales_all", tag="x_second", align_bytes=MX_ALIGN)
+        nc.sync.dma_start(out=x_scales_all[0:scale_rows, :].bitcast(I32), in_=x_scales.rearrange("o b n -> b o n").bitcast(I32))
+        offs_list = sb.tile([P, S // 16], U16, name="offs_list")
+        nc.sync.dma_start(offs_list[:], offs)
+        h_rows = hT.rearrange("(o p r) i -> o p r i", o=PASSES, r=PACK)
+        h_raw = [sb.tile([P, PACK, H], F32, name=f"h_raw{o}", tag=f"h_raw{o}") for o in range(PASSES)]
         for o in range(PASSES):
-            nc.sync.dma_start(out=xw_all[o][:].bitcast(I32), in_=x_words[o].rearrange("p n r -> p (n r)").bitcast(I32))
-        nc.sync.dma_start(out=w_raw[:], in_=w1.rearrange("(p j) m -> p j m", j=PACK))
-        nc.sync.dma_start(rec_t[:], rec)
+            nc.sync.dma_start(out=h_raw[o][:], in_=h_rows[o])
+        x_rows = x_words.rearrange("o p n r -> o p (n r)").bitcast(I32)
+        x_words_all = [sb.tile([P, T], U32, name="x_words_all0", align_bytes=MX_ALIGN)]
+        nc.sync.dma_start(out=x_words_all[0][:].bitcast(I32), in_=x_rows[0])
+        rec_list = sb.tile([P, S // 16], U16, name="rec_list")
+        nc.sync.dma_start(rec_list[:], rec)
+
+        nc.vector.memset(x_scales_all[scale_rows:64, :].bitcast(I32), 0)
+        nc.vector.memset(x_scales_all[64:P, :].bitcast(I32), 0)
+        x_scales_picked = sb.tile([P, S], U8, name="x_scales_picked", align_bytes=MX_ALIGN)
+        nc.vector.tensor_copy(x_scales_picked[:], x_scales_all[:].indirect(offs_list[:]))
+        x_plane = sb.tile([P, PASSES, S], U8, name="x_plane", align_bytes=MX_ALIGN)
+        for q in range(P // 32):
+            nc.sync.dma_start(out=x_plane[32 * q : 32 * q + 4, :, :].bitcast(I32), in_=x_scales_picked[8 * q : 8 * q + 8, :].bitcast(I32))
+        x_words_all.append(sb.tile([P, T], U32, name="x_words_all1", tag="x_second", align_bytes=MX_ALIGN))
+        nc.sync.dma_start(out=x_words_all[1][:].bitcast(I32), in_=x_rows[1])
+
+        h_codes = [sb.tile([P, H], U32, name=f"h_codes{o}", align_bytes=MX_ALIGN) for o in range(PASSES)]
+        h_scales = [sb.tile([P, H], U8, name=f"h_scales{o}", align_bytes=MX_ALIGN) for o in range(PASSES)]
+        for o in range(PASSES):
+            dealt = h_raw[o][:].rearrange("p r (m t) -> p m t r", t=PACK)
+            for first_slab in (0, 2):
+                h_bf = sb.tile([P, 2, P, PACK], BF16, name=f"h_bf{o}{first_slab}", align_bytes=MX_ALIGN)
+                target = h_bf[:].rearrange("p t m r -> p m t r")
+                source = dealt[:, :, first_slab : first_slab + 2, :]
+                if first_slab == 0:
+                    nc.vector.tensor_copy(out=target, in_=source)
+                else:
+                    nc.scalar.activation(target, source, ACT.Copy)
+                cols = slice(P * first_slab, P * (first_slab + 2))
+                quantise(h_bf[:].rearrange("p t m r -> p (t m r)"), h_codes[o][:, cols], h_scales[o][:, cols])
+
+        later = sb.tile([P, (PACK + 1) * S + PACK], F32, name="later", tag="h_raw0")
+        sw_slab = [later[:, S * t : S * (t + 1)] for t in range(PACK)]
+        w_raw = later[:, PACK * S : (PACK + 1) * S].rearrange("p (t m) -> p t m", t=PACK)
+        unit_cols = later[:, (PACK + 1) * S :]
+        nc.sync.dma_start(out=w_raw, in_=w1.rearrange("(p t) m -> p t m", t=PACK))
         sw_rows = sw.rearrange("(p t) j -> p t j", t=PACK)
         for t in range(PACK):
-            nc.sync.dma_start(out=sw_t[t][:], in_=sw_rows[:, t, :])
-        nc.sync.dma_start(out=unit_t[:], in_=unit.rearrange("(p t) o -> p (t o)", t=PACK))
+            nc.sync.dma_start(out=sw_slab[t], in_=sw_rows[:, t, :])
+        nc.sync.dma_start(out=unit_cols, in_=unit.rearrange("(p t) o -> p (t o)", t=PACK))
 
-        xs_picked = sb.tile([P, S], U8, name="xs_picked", align_bytes=64)
-        nc.vector.tensor_copy(xs_picked[:], xs_all[:].indirect(offs_t[:]))
-        xs = sb.tile([P, PASSES, S], U8, name="xs", align_bytes=64)
-        for q in range(4):
-            nc.gpsimd.dma_start(out=xs[32 * q : 32 * q + 4, :, :].bitcast(I32), in_=xs_picked[8 * q : 8 * q + 8, :].bitcast(I32))
-
-        h_codes = [sb.tile([P, H], U32, name=f"h_codes{o}", align_bytes=64) for o in range(PASSES)]
-        h_scales = [sb.tile([P, H], U8, name=f"h_scales{o}", align_bytes=64) for o in range(PASSES)]
-        for o in range(PASSES):
-            src = h_raw[o][:].rearrange("p j (m t) -> p m j t", t=PACK)
-            for half in range(2):
-                h_bf = sb.tile([P, 2, P, PACK], BF16, name=f"h_bf{o}{half}", align_bytes=64)
-                dst = h_bf[:].rearrange("p t m j -> p m j t")
-                if half == 0:
-                    nc.vector.tensor_copy(out=dst, in_=src[:, :, :, 0:2])
-                else:
-                    nc.scalar.activation(dst, src[:, :, :, 2:4], ACT.Copy)
-                cols = slice(256 * half, 256 * (half + 1))
-                nc.vector.quantize_mx(
-                    out=h_codes[o][:, cols].bitcast(FP8X4),
-                    scales=h_scales[o][:, cols],
-                    in_=h_bf[:].rearrange("p t m j -> p (t m j)"),
-                )
-
-        xw = [sb.tile([P, S], U32, name=f"xw{o}", align_bytes=64) for o in range(PASSES)]
-        halves = [slice(0, S // 2), slice(S // 2, S)]
-        pieces = [(0, halves[0]), (0, halves[1])] + [(t, slice(0, S)) for t in range(1, PACK)]
-        y = [psum.tile([P, c.stop - c.start], F32, name=f"y{n}") for n, (t, c) in enumerate(pieces)]
+        x_picked = [sb.tile([P, S], U32, name=f"x_picked{o}", align_bytes=MX_ALIGN) for o in range(PASSES)]
         for o in range(PASSES):
             for h in range(2):
-                nc.vector.tensor_copy(xw[o][:, halves[h]], xw_all[o][:].indirect(offs_t[:, 16 * h : 16 * (h + 1)]))
-        for n, (t, c) in enumerate(pieces):
+                nc.vector.tensor_copy(x_picked[o][:, ENTRIES[h]], x_words_all[o][:].indirect(offs_list[:, LIST_COLUMNS[h]]))
+        y_parts = [(0, ENTRIES[0]), (0, ENTRIES[1])] + [(t, slice(0, S)) for t in range(1, PACK)]
+        y = [psum.tile([P, c.stop - c.start], F32, name=f"y{n}") for n, (t, c) in enumerate(y_parts)]
+        for n, (t, c) in enumerate(y_parts):
             cols = slice(P * t, P * (t + 1))
-            for o in range(PASSES):
+            order = (1, 0) if t == PACK - 1 else (0, 1)
+            for o in order:
                 nc.tensor.matmul_mx(
                     out=y[n][:],
                     lhsT=h_codes[o][:, cols].bitcast(FP8X4),
                     lhsT_scale=h_scales[o][:, cols],
-                    rhs=xw[o][:, c].bitcast(FP8X4),
-                    rhs_scale=xs[:, o, c],
-                    start=(o == 0),
-                    stop=(o == PASSES - 1),
+                    rhs=x_picked[o][:, c].bitcast(FP8X4),
+                    rhs_scale=x_plane[:, o, c],
+                    start=(o == order[0]),
+                    stop=(o == order[-1]),
                 )
 
-        w_bf = sb.tile([P, N, PACK], BF16, name="w_bf", align_bytes=64)
-        nc.vector.tensor_copy(
-            w_bf[:].rearrange("p (c i) j -> p c j i", i=4), w_raw[:].rearrange("p j (c i) -> p c j i", i=4)
-        )
-        w_codes = sb.tile([P, N], U32, name="w_codes", align_bytes=64)
-        w_scales = sb.tile([P, N], U8, name="w_scales", align_bytes=64)
-        nc.vector.quantize_mx(out=w_codes[:].bitcast(FP8X4), scales=w_scales[:], in_=w_bf[:].rearrange("p m j -> p (m j)"))
+        w_bf = sb.tile([P, N, PACK], BF16, name="w_bf", align_bytes=MX_ALIGN)
+        nc.vector.tensor_copy(w_bf[:].rearrange("p (c n) t -> p c t n", n=4), w_raw.rearrange("p t (c n) -> p c t n", n=4))
+        w_codes = sb.tile([P, N], U32, name="w_codes", align_bytes=MX_ALIGN)
+        w_scales = sb.tile([P, N], U8, name="w_scales", align_bytes=MX_ALIGN)
+        quantise(w_bf[:].rearrange("p m t -> p (m t)"), w_codes[:], w_scales[:])
 
         total = sb.tile([P, PACK], F32, name="total")
         post = sb.tile([P, PACK, S], F32, name="post")
         den = sb.tile([P, PACK, GROUPS], F32, name="den")
-        vhalves = [slice(0, GROUPS // 2), slice(GROUPS // 2, GROUPS)]
-        on_vector = [(0, 0), (0, 1)]
-        for t in range(PACK):
-            col = slice(t, t + 1)
-            th = sb.tile([P, S], F32, name=f"th{t}")
-            em = sb.tile([P, S], F32, name=f"em{t}")
-            for n, (tn, c) in enumerate(pieces):
-                if tn == t:
-                    nc.scalar.activation(th[:, c], y[n][:], ACT.Tanh)
-            nc.scalar.activation(em[:], th[:], ACT.Exp, scale=1.1, accum_out=total[:, col])
-            if t == 0:
-                avg = sb.tile([P, 1], F32, name="avg")
-                nc.vector.tensor_scalar(avg[:], total[:, col], 1.0 / S, None, ALU.mult)
-            stay = sb.tile([P, S], F32, name=f"stay{t}")
-            er = sb.tile([P, S], F32, name=f"er{t}")
-            kept = sb.tile([P, S], F32, name=f"kept{t}")
-            pairs = sb.tile([P, GROUPS, 2], F32, name=f"pairs{t}")
-            quads = post[:, t, :].rearrange("p (v d) -> p v d", d=D)
-            if t == 0:
-                nc.vector.tensor_scalar(stay[:], sw_t[t][:], -float(S), float(S), ALU.mult, ALU.add)
-            else:
-                nc.vector.tensor_scalar(stay[:], sw_t[t][:], -1.0, 1.0, ALU.mult, ALU.add)
-            for h in range(2):
-                picked = em[:].indirect(rec_t[:, 16 * h : 16 * (h + 1)])
-                if (t, h) in on_vector:
-                    nc.vector.tensor_copy(er[:, halves[h]], picked)
-                else:
-                    nc.scalar.activation(er[:, halves[h]], picked, ACT.Copy, scale=float(S))
-            for h, c in enumerate(halves):
-                centre = avg[:] if (t, h) in on_vector else total[:, col]
-                nc.vector.scalar_tensor_tensor(kept[:, c], er[:, c], centre, stay[:, c], ALU.subtract, ALU.mult)
-            for c in halves:
-                nc.vector.scalar_tensor_tensor(post[:, t, c], kept[:, c], total[:, col], em[:, c], ALU.add, ALU.mult)
-            for v in vhalves:
-                nc.vector.tensor_tensor(pairs[:, v, :], quads[:, v, 0:2], quads[:, v, 2:4], ALU.add)
-            for v in vhalves:
-                nc.vector.scalar_tensor_tensor(den[:, t, v], pairs[:, v, 0], 0.2 * S, pairs[:, v, 1], ALU.add, ALU.add)
+        em, avg, stay, er, kept, pair_sums = {}, {}, {}, {}, {}, {}
 
-        sign = sb.tile([P, PACK, GROUPS], F32, name="sign")
+        def emission(t):
+            th = sb.tile([P, S], F32, name=f"th{t}")
+            em[t] = sb.tile([P, S], F32, name=f"em{t}")
+            for n, (slab, c) in enumerate(y_parts):
+                if slab == t:
+                    nc.scalar.activation(th[:, c], y[n][:], ACT.Tanh)
+            nc.scalar.activation(em[t][:], th[:], ACT.Exp, scale=1.1, accum_out=total[:, t : t + 1])
+            scaled = [(t, h) in VECTOR_LOOKUPS for h in range(2)]
+            if any(scaled):
+                avg[t] = sb.tile([P, 1], F32, name=f"avg{t}")
+                nc.vector.tensor_scalar(avg[t][:], total[:, t : t + 1], 1.0 / S, None, ALU.mult)
+            stay[t] = sb.tile([P, S], F32, name=f"stay{t}")
+            spans = [(slice(0, S), scaled[0])] if scaled[0] == scaled[1] else list(zip(ENTRIES, scaled))
+            for c, times_s in spans:
+                one = float(S) if times_s else 1.0
+                nc.vector.tensor_scalar(stay[t][:, c], sw_slab[t][:, c], -one, one, ALU.mult, ALU.add)
+            er[t] = sb.tile([P, S], F32, name=f"er{t}")
+            kept[t] = sb.tile([P, S], F32, name=f"kept{t}")
+            pair_sums[t] = sb.tile([P, GROUPS, 2], F32, name=f"pair_sums{t}")
+
+        for pieces in PIECE_PAIRS:
+            for t, h in pieces:
+                if t not in em:
+                    emission(t)
+                looked_up = em[t][:].indirect(rec_list[:, LIST_COLUMNS[h]])
+                if (t, h) in VECTOR_LOOKUPS:
+                    nc.vector.tensor_copy(er[t][:, ENTRIES[h]], looked_up)
+                else:
+                    nc.scalar.activation(er[t][:, ENTRIES[h]], looked_up, ACT.Copy, scale=float(S))
+            for t, h in pieces:
+                c = ENTRIES[h]
+                centre = avg[t][:] if (t, h) in VECTOR_LOOKUPS else total[:, t : t + 1]
+                nc.vector.scalar_tensor_tensor(kept[t][:, c], er[t][:, c], centre, stay[t][:, c], ALU.subtract, ALU.mult)
+            for t, h in pieces:
+                c = ENTRIES[h]
+                nc.vector.scalar_tensor_tensor(post[:, t, c], kept[t][:, c], total[:, t : t + 1], em[t][:, c], ALU.add, ALU.mult)
+            for t, h in pieces:
+                v = GROUP_HALVES[h]
+                quads = post[:, t, :].rearrange("p (v d) -> p v d", d=D)
+                nc.vector.tensor_tensor(pair_sums[t][:, v, :], quads[:, v, 0:2], quads[:, v, 2:4], ALU.add)
+            for t, h in pieces:
+                v = GROUP_HALVES[h]
+                nc.vector.scalar_tensor_tensor(den[:, t, v], pair_sums[t][:, v, 0], 0.2 * S, pair_sums[t][:, v, 1], ALU.add, ALU.add)
+
         root = sb.tile([P, PACK, GROUPS], F32, name="root")
-        inv = sb.tile([P, PACK, GROUPS], F32, name="inv")
+        sign = sb.tile([P, PACK, GROUPS], F32, name="sign")
+        inverse = sb.tile([P, PACK, GROUPS], F32, name="inverse")
+        for v in GROUP_HALVES:
+            nc.scalar.activation(root[:, :, v], den[:, :, v], ACT.Abs_reciprocal_sqrt)
+            nc.scalar.activation(sign[:, :, v], den[:, :, v], ACT.Sign)
+            nc.scalar.activation(inverse[:, :, v], root[:, :, v], ACT.Square)
+
         factor = sb.tile([P, PACK, GROUPS], F32, name="factor")
-        for vs in vhalves:
-            nc.scalar.activation(root[:, :, vs], den[:, :, vs], ACT.Abs_reciprocal_sqrt)
-            nc.scalar.activation(sign[:, :, vs], den[:, :, vs], ACT.Sign)
-            nc.scalar.activation(inv[:, :, vs], root[:, :, vs], ACT.Square)
-        for c, cols in enumerate([slice(0, 256), slice(256, 384), slice(384, 512)]):
+        for n, cols in enumerate(OUT_CHUNKS):
             width = cols.stop - cols.start
-            vs = slice(cols.start // D, cols.stop // D)
-            if c < 2:
-                for t in range(PACK):
-                    v = vhalves[c]
-                    nc.vector.scalar_tensor_tensor(factor[:, t, v], inv[:, t, v], unit_t[:, t : t + 1], sign[:, t, v], ALU.mult, ALU.mult)
-            hid = sb.tile([P, width, PACK], BF16, name=f"hid{c}", align_bytes=64)
+            for c, v in zip(ENTRIES, GROUP_HALVES):
+                if c.start == cols.start:
+                    for t in range(PACK):
+                        nc.vector.scalar_tensor_tensor(factor[:, t, v], inverse[:, t, v], unit_cols[:, t : t + 1], sign[:, t, v], ALU.mult, ALU.mult)
+            groups = slice(cols.start // D, cols.stop // D)
+            hid = sb.tile([P, width, PACK], BF16, name=f"hid{n}", align_bytes=MX_ALIGN)
             nc.vector.tensor_tensor(
                 hid[:].rearrange("p (v d) t -> p v t d", d=D),
                 post[:, :, cols].rearrange("p t (v d) -> p v t d", d=D),
-                factor[:, :, vs].rearrange("p t v -> p v t").unsqueeze(3).to_broadcast([P, width // D, PACK, D]),
+                factor[:, :, groups].rearrange("p t v -> p v t").unsqueeze(3).to_broadcast([P, width // D, PACK, D]),
                 ALU.mult,
             )
-            hid_codes = sb.tile([P, width], U32, name=f"hid_codes{c}", align_bytes=64)
-            hid_scales = sb.tile([P, width], U8, name=f"hid_scales{c}", align_bytes=64)
-            nc.vector.quantize_mx(out=hid_codes[:].bitcast(FP8X4), scales=hid_scales[:], in_=hid[:].rearrange("p j t -> p (j t)"))
-            acc = psum.tile([P, width], F32, name=f"acc{c}")
+            hid_codes = sb.tile([P, width], U32, name=f"hid_codes{n}", align_bytes=MX_ALIGN)
+            hid_scales = sb.tile([P, width], U8, name=f"hid_scales{n}", align_bytes=MX_ALIGN)
+            quantise(hid[:].rearrange("p j t -> p (j t)"), hid_codes[:], hid_scales[:])
+            acc = psum.tile([P, width], F32, name=f"acc{n}")
             nc.tensor.matmul_mx(
                 out=acc[:],
                 lhsT=w_codes[:].bitcast(FP8X4),
@@ -180,6 +201,6 @@ def tile_picked_ypopgn_post_p_kernel(tc, x_words, x_scales, hT, sw, unit, w1, of
                 start=True,
                 stop=True,
             )
-            res = sb.tile([P, width], F32, name=f"res{c}")
-            nc.scalar.copy(res[:], acc[:])
-            nc.sync.dma_start(out=out[:, cols], in_=res[:])
+            result = sb.tile([P, width], F32, name=f"result{n}")
+            nc.scalar.copy(result[:], acc[:])
+            nc.sync.dma_start(out=out[:, cols], in_=result[:])

from contextlib import ExitStack

import concourse.mybir as mybir

K, T, S, D, N, H = 1024, 2048, 512, 4, 128, 512
FLOPS = 2 * K * H * S + 2 * H * N * S

F32 = mybir.dt.float32
BF16 = mybir.dt.bfloat16
I32 = mybir.dt.int32
U32 = mybir.dt.uint32
U16 = mybir.dt.uint16
U8 = mybir.dt.uint8
FP8X4 = mybir.dt.float8_e4m3fn_x4
ACT = mybir.ActivationFunctionType
ALU = mybir.AluOpType

P = 128
PACK = 4
PASSES = K // (P * PACK)
BLOCKS = P * PACK // 32
GROUPS = S // D
MX_ALIGN = 64

ENTRIES = [slice(0, S // 2), slice(S // 2, S)]
LIST_COLUMNS = [slice(0, S // 32), slice(S // 32, S // 16)]
GROUP_HALVES = [slice(0, GROUPS // 2), slice(GROUPS // 2, GROUPS)]

PIECE_PAIRS = [[(0, 0), (0, 1)], [(1, 0), (1, 1)], [(2, 0), (3, 0)], [(2, 1), (3, 1)]]
VECTOR_LOOKUPS = [(0, 0), (0, 1), (1, 0)]
OUT_CHUNKS = [slice(0, 256), slice(256, 384), slice(384, 512)]


def tile_picked_ypopgn_post_p_kernel(tc, x_words, x_scales, hT, sw, unit, w1, offs, rec, out):
    nc = tc.nc
    with ExitStack() as ctx:
        sb = ctx.enter_context(tc.tile_pool(name="sb", bufs=1))
        psum = ctx.enter_context(tc.psum_pool(name="psum", bufs=1))

        def quantise(values, codes, scales):
            nc.vector.quantize_mx(out=codes.bitcast(FP8X4), scales=scales, in_=values)

        scale_rows = PASSES * BLOCKS
        x_scales_all = sb.tile([P, T], U8, name="x_scales_all", tag="x_second", align_bytes=MX_ALIGN)
        nc.sync.dma_start(out=x_scales_all[0:scale_rows, :].bitcast(I32), in_=x_scales.rearrange("o b n -> b o n").bitcast(I32))
        offs_list = sb.tile([P, S // 16], U16, name="offs_list")
        nc.sync.dma_start(offs_list[:], offs)
        h_rows = hT.rearrange("(o p r) i -> o p r i", o=PASSES, r=PACK)
        h_raw = [sb.tile([P, PACK, H], F32, name=f"h_raw{o}", tag=f"h_raw{o}") for o in range(PASSES)]
        for o in range(PASSES):
            nc.sync.dma_start(out=h_raw[o][:], in_=h_rows[o])
        x_rows = x_words.rearrange("o p n r -> o p (n r)").bitcast(I32)
        x_words_all = [sb.tile([P, T], U32, name="x_words_all0", align_bytes=MX_ALIGN)]
        nc.sync.dma_start(out=x_words_all[0][:].bitcast(I32), in_=x_rows[0])
        rec_list = sb.tile([P, S // 16], U16, name="rec_list")
        nc.sync.dma_start(rec_list[:], rec)

        nc.vector.memset(x_scales_all[scale_rows:64, :].bitcast(I32), 0)
        nc.vector.memset(x_scales_all[64:P, :].bitcast(I32), 0)
        x_scales_picked = sb.tile([P, S], U8, name="x_scales_picked", align_bytes=MX_ALIGN)
        nc.vector.tensor_copy(x_scales_picked[:], x_scales_all[:].indirect(offs_list[:]))
        x_plane = sb.tile([P, PASSES, S], U8, name="x_plane", align_bytes=MX_ALIGN)
        for q in range(P // 32):
            nc.sync.dma_start(out=x_plane[32 * q : 32 * q + 4, :, :].bitcast(I32), in_=x_scales_picked[8 * q : 8 * q + 8, :].bitcast(I32))
        x_words_all.append(sb.tile([P, T], U32, name="x_words_all1", tag="x_second", align_bytes=MX_ALIGN))
        nc.sync.dma_start(out=x_words_all[1][:].bitcast(I32), in_=x_rows[1])

        h_codes = [sb.tile([P, H], U32, name=f"h_codes{o}", align_bytes=MX_ALIGN) for o in range(PASSES)]
        h_scales = [sb.tile([P, H], U8, name=f"h_scales{o}", align_bytes=MX_ALIGN) for o in range(PASSES)]
        for o in range(PASSES):
            dealt = h_raw[o][:].rearrange("p r (m t) -> p m t r", t=PACK)
            for first_slab in (0, 2):
                h_bf = sb.tile([P, 2, P, PACK], BF16, name=f"h_bf{o}{first_slab}", align_bytes=MX_ALIGN)
                target = h_bf[:].rearrange("p t m r -> p m t r")
                source = dealt[:, :, first_slab : first_slab + 2, :]
                if first_slab == 0:
                    nc.vector.tensor_copy(out=target, in_=source)
                else:
                    nc.scalar.activation(target, source, ACT.Copy)
                cols = slice(P * first_slab, P * (first_slab + 2))
                quantise(h_bf[:].rearrange("p t m r -> p (t m r)"), h_codes[o][:, cols], h_scales[o][:, cols])

        later = sb.tile([P, (PACK + 1) * S + PACK], F32, name="later", tag="h_raw0")
        sw_slab = [later[:, S * t : S * (t + 1)] for t in range(PACK)]
        w_raw = later[:, PACK * S : (PACK + 1) * S].rearrange("p (t m) -> p t m", t=PACK)
        unit_cols = later[:, (PACK + 1) * S :]
        nc.sync.dma_start(out=w_raw, in_=w1.rearrange("(p t) m -> p t m", t=PACK))
        sw_rows = sw.rearrange("(p t) j -> p t j", t=PACK)
        for t in range(PACK):
            nc.sync.dma_start(out=sw_slab[t], in_=sw_rows[:, t, :])
        nc.sync.dma_start(out=unit_cols, in_=unit.rearrange("(p t) o -> p (t o)", t=PACK))

        x_picked = [sb.tile([P, S], U32, name=f"x_picked{o}", align_bytes=MX_ALIGN) for o in range(PASSES)]
        for o in range(PASSES):
            for h in range(2):
                nc.vector.tensor_copy(x_picked[o][:, ENTRIES[h]], x_words_all[o][:].indirect(offs_list[:, LIST_COLUMNS[h]]))
        y_parts = [(0, ENTRIES[0]), (0, ENTRIES[1])] + [(t, slice(0, S)) for t in range(1, PACK)]
        y = [psum.tile([P, c.stop - c.start], F32, name=f"y{n}") for n, (t, c) in enumerate(y_parts)]
        for n, (t, c) in enumerate(y_parts):
            cols = slice(P * t, P * (t + 1))
            order = (1, 0) if t == PACK - 1 else (0, 1)
            for o in order:
                nc.tensor.matmul_mx(
                    out=y[n][:],
                    lhsT=h_codes[o][:, cols].bitcast(FP8X4),
                    lhsT_scale=h_scales[o][:, cols],
                    rhs=x_picked[o][:, c].bitcast(FP8X4),
                    rhs_scale=x_plane[:, o, c],
                    start=(o == order[0]),
                    stop=(o == order[-1]),
                )

        w_bf = sb.tile([P, N, PACK], BF16, name="w_bf", align_bytes=MX_ALIGN)
        nc.vector.tensor_copy(w_bf[:].rearrange("p (c n) t -> p c t n", n=4), w_raw.rearrange("p t (c n) -> p c t n", n=4))
        w_codes = sb.tile([P, N], U32, name="w_codes", align_bytes=MX_ALIGN)
        w_scales = sb.tile([P, N], U8, name="w_scales", align_bytes=MX_ALIGN)
        quantise(w_bf[:].rearrange("p m t -> p (m t)"), w_codes[:], w_scales[:])

        total = sb.tile([P, PACK], F32, name="total")
        post = sb.tile([P, PACK, S], F32, name="post")
        den = sb.tile([P, PACK, GROUPS], F32, name="den")
        em, avg, stay, er, kept, pair_sums = {}, {}, {}, {}, {}, {}

        def emission(t):
            th = sb.tile([P, S], F32, name=f"th{t}")
            em[t] = sb.tile([P, S], F32, name=f"em{t}")
            for n, (slab, c) in enumerate(y_parts):
                if slab == t:
                    nc.scalar.activation(th[:, c], y[n][:], ACT.Tanh)
            nc.scalar.activation(em[t][:], th[:], ACT.Exp, scale=1.1, accum_out=total[:, t : t + 1])
            scaled = [(t, h) in VECTOR_LOOKUPS for h in range(2)]
            if any(scaled):
                avg[t] = sb.tile([P, 1], F32, name=f"avg{t}")
                nc.vector.tensor_scalar(avg[t][:], total[:, t : t + 1], 1.0 / S, None, ALU.mult)
            stay[t] = sb.tile([P, S], F32, name=f"stay{t}")
            spans = [(slice(0, S), scaled[0])] if scaled[0] == scaled[1] else list(zip(ENTRIES, scaled))
            for c, times_s in spans:
                one = float(S) if times_s else 1.0
                nc.vector.tensor_scalar(stay[t][:, c], sw_slab[t][:, c], -one, one, ALU.mult, ALU.add)
            er[t] = sb.tile([P, S], F32, name=f"er{t}")
            kept[t] = sb.tile([P, S], F32, name=f"kept{t}")
            pair_sums[t] = sb.tile([P, GROUPS, 2], F32, name=f"pair_sums{t}")

        for pieces in PIECE_PAIRS:
            for t, h in pieces:
                if t not in em:
                    emission(t)
                looked_up = em[t][:].indirect(rec_list[:, LIST_COLUMNS[h]])
                if (t, h) in VECTOR_LOOKUPS:
                    nc.vector.tensor_copy(er[t][:, ENTRIES[h]], looked_up)
                else:
                    nc.scalar.activation(er[t][:, ENTRIES[h]], looked_up, ACT.Copy, scale=float(S))
            for t, h in pieces:
                c = ENTRIES[h]
                centre = avg[t][:] if (t, h) in VECTOR_LOOKUPS else total[:, t : t + 1]
                nc.vector.scalar_tensor_tensor(kept[t][:, c], er[t][:, c], centre, stay[t][:, c], ALU.subtract, ALU.mult)
            for t, h in pieces:
                c = ENTRIES[h]
                nc.vector.scalar_tensor_tensor(post[:, t, c], kept[t][:, c], total[:, t : t + 1], em[t][:, c], ALU.add, ALU.mult)
            for t, h in pieces:
                v = GROUP_HALVES[h]
                quads = post[:, t, :].rearrange("p (v d) -> p v d", d=D)
                nc.vector.tensor_tensor(pair_sums[t][:, v, :], quads[:, v, 0:2], quads[:, v, 2:4], ALU.add)
            for t, h in pieces:
                v = GROUP_HALVES[h]
                nc.vector.scalar_tensor_tensor(den[:, t, v], pair_sums[t][:, v, 0], 0.2 * S, pair_sums[t][:, v, 1], ALU.add, ALU.add)

        root = sb.tile([P, PACK, GROUPS], F32, name="root")
        sign = sb.tile([P, PACK, GROUPS], F32, name="sign")
        inverse = sb.tile([P, PACK, GROUPS], F32, name="inverse")
        for v in GROUP_HALVES:
            nc.scalar.activation(root[:, :, v], den[:, :, v], ACT.Abs_reciprocal_sqrt)
            nc.scalar.activation(sign[:, :, v], den[:, :, v], ACT.Sign)
            nc.scalar.activation(inverse[:, :, v], root[:, :, v], ACT.Square)

        factor = sb.tile([P, PACK, GROUPS], F32, name="factor")
        for n, cols in enumerate(OUT_CHUNKS):
            width = cols.stop - cols.start
            for c, v in zip(ENTRIES, GROUP_HALVES):
                if c.start == cols.start:
                    for t in range(PACK):
                        nc.vector.scalar_tensor_tensor(factor[:, t, v], inverse[:, t, v], unit_cols[:, t : t + 1], sign[:, t, v], ALU.mult, ALU.mult)
            groups = slice(cols.start // D, cols.stop // D)
            hid = sb.tile([P, width, PACK], BF16, name=f"hid{n}", align_bytes=MX_ALIGN)
            nc.vector.tensor_tensor(
                hid[:].rearrange("p (v d) t -> p v t d", d=D),
                post[:, :, cols].rearrange("p t (v d) -> p v t d", d=D),
                factor[:, :, groups].rearrange("p t v -> p v t").unsqueeze(3).to_broadcast([P, width // D, PACK, D]),
                ALU.mult,
            )
            hid_codes = sb.tile([P, width], U32, name=f"hid_codes{n}", align_bytes=MX_ALIGN)
            hid_scales = sb.tile([P, width], U8, name=f"hid_scales{n}", align_bytes=MX_ALIGN)
            quantise(hid[:].rearrange("p j t -> p (j t)"), hid_codes[:], hid_scales[:])
            acc = psum.tile([P, width], F32, name=f"acc{n}")
            nc.tensor.matmul_mx(
                out=acc[:],
                lhsT=w_codes[:].bitcast(FP8X4),
                lhsT_scale=w_scales[:],
                rhs=hid_codes[:].bitcast(FP8X4),
                rhs_scale=hid_scales[:],
                start=True,
                stop=True,
            )
            result = sb.tile([P, width], F32, name=f"result{n}")
            nc.scalar.copy(result[:], acc[:])
            nc.sync.dma_start(out=out[:, cols], in_=result[:])
